import numpy as np
CORES = [0,1,2,3,4,5,6,7]
N = 8
GROUPS = [[0,4],[1,5],[2,6],[3,7]]
def setup_inputs(rng):
    return {"x": rng.standard_normal((N, 128, 1024), dtype=np.float32)}
def reference(x):
    y = np.empty((N, 128, 1024), x.dtype)
    for g in GROUPS:
        s = x[g].sum(axis=0, dtype=np.float64).astype(x[g].dtype)
        for r in g:
            y[r] = s
    return {"y": y}

@@ -1,0 +1,56 @@
+from concourse.mybir import AluOpType
+
+COLS = 1024
+NBLK = 1
+MAXPEERS = 1
+
+SCRATCH = {"mine": ("sbuf", [128, COLS], "float32")}
+for _j in range(MAXPEERS):
+    SCRATCH["land%d" % _j] = ("sbuf", [128, COLS], "float32")
+
+SEMAPHORES = ["seed", "sent"]
+SEMAPHORES += ["ld%d" % k for k in range(NBLK)]
+SEMAPHORES += ["acc%d" % k for k in range(NBLK)]
+SEMAPHORES += ["arr%d_%d" % (j, k) for j in range(MAXPEERS) for k in range(NBLK)]
+
+
+def rank_program(g, core, T, topo):
+    rank = T.rank_of(core)
+    if rank is None:
+        return
+    group = [grp for grp in T.tables["GROUPS"] if rank in grp][0]
+    peers = [r for r in group if r != rank]
+    w = COLS // NBLK
+    blocks = [slice(k * w, (k + 1) * w) for k in range(NBLK)]
+
+    g.scalar.dma_start(T.y[:, :], T.x[:, :]).then_inc(T.sem.seed, 16)
+
+    for k, b in enumerate(blocks):
+        g.sync.dma_start(T.mine[:, b], T.x[:, b]).then_inc(T.sem["ld%d" % k], 16)
+
+    nsent = 0
+    for k, b in enumerate(blocks):
+        g.wait_ge(T.sem["ld%d" % k], 16)
+        for p in peers:
+            dst = T.cores[p]
+            slot = [r for r in group if r != p].index(rank)
+            rid, pid, _se = topo.addr(dst)
+            g.remote_dma(
+                T["land%d" % slot][:, b], T.mine[:, b],
+                T.sem["arr%d_%d" % (slot, k)], T.sem.sent,
+                pid, rid, topo.mask(core, dst),
+            )
+            nsent += 16
+
+    g.wait_ge(T.sem.seed, 16)
+    for j in range(len(peers)):
+        for k, b in enumerate(blocks):
+            g.wait_ge(T.sem["arr%d_%d" % (j, k)], 16)
+            if j > 0:
+                g.wait_ge(T.sem["acc%d" % k], 16 * j)
+            g.dma_start(T.y[:, b], T["land%d" % j][:, b], accum_op=AluOpType.add).then_inc(
+                T.sem["acc%d" % k], 16)
+
+    for k in range(NBLK):
+        g.wait_ge(T.sem["acc%d" % k], 16 * len(peers))
+    g.wait_ge(T.sem.sent, nsent)

@@ -1,56 +1,29 @@
 from concourse.mybir import AluOpType
 
-COLS = 1024
-NBLK = 1
-MAXPEERS = 1
-
-SCRATCH = {"mine": ("sbuf", [128, COLS], "float32")}
-for _j in range(MAXPEERS):
-    SCRATCH["land%d" % _j] = ("sbuf", [128, COLS], "float32")
-
-SEMAPHORES = ["seed", "sent"]
-SEMAPHORES += ["ld%d" % k for k in range(NBLK)]
-SEMAPHORES += ["acc%d" % k for k in range(NBLK)]
-SEMAPHORES += ["arr%d_%d" % (j, k) for j in range(MAXPEERS) for k in range(NBLK)]
+SCRATCH = {
+    "mine": ("sbuf", [128, 1024], "float32"),
+    "land": ("sbuf", [128, 1024], "float32"),
+}
+SEMAPHORES = ["seed", "staged", "sent", "arrived", "added"]
 
 
 def rank_program(g, core, T, topo):
     rank = T.rank_of(core)
     if rank is None:
         return
-    group = [grp for grp in T.tables["GROUPS"] if rank in grp][0]
-    peers = [r for r in group if r != rank]
-    w = COLS // NBLK
-    blocks = [slice(k * w, (k + 1) * w) for k in range(NBLK)]
+    pair = [grp for grp in T.tables["GROUPS"] if rank in grp][0]
+    partner = T.cores[[r for r in pair if r != rank][0]]
+    rid, pid, _se = topo.addr(partner)
 
     g.scalar.dma_start(T.y[:, :], T.x[:, :]).then_inc(T.sem.seed, 16)
 
-    for k, b in enumerate(blocks):
-        g.sync.dma_start(T.mine[:, b], T.x[:, b]).then_inc(T.sem["ld%d" % k], 16)
-
-    nsent = 0
-    for k, b in enumerate(blocks):
-        g.wait_ge(T.sem["ld%d" % k], 16)
-        for p in peers:
-            dst = T.cores[p]
-            slot = [r for r in group if r != p].index(rank)
-            rid, pid, _se = topo.addr(dst)
-            g.remote_dma(
-                T["land%d" % slot][:, b], T.mine[:, b],
-                T.sem["arr%d_%d" % (slot, k)], T.sem.sent,
-                pid, rid, topo.mask(core, dst),
-            )
-            nsent += 16
+    g.sync.dma_start(T.mine[:, :], T.x[:, :]).then_inc(T.sem.staged, 16)
+    g.wait_ge(T.sem.staged, 16)
+    g.remote_dma(T.land[:, :], T.mine[:, :], T.sem.arrived, T.sem.sent, pid, rid, topo.mask(core, partner))
 
     g.wait_ge(T.sem.seed, 16)
-    for j in range(len(peers)):
-        for k, b in enumerate(blocks):
-            g.wait_ge(T.sem["arr%d_%d" % (j, k)], 16)
-            if j > 0:
-                g.wait_ge(T.sem["acc%d" % k], 16 * j)
-            g.dma_start(T.y[:, b], T["land%d" % j][:, b], accum_op=AluOpType.add).then_inc(
-                T.sem["acc%d" % k], 16)
+    g.wait_ge(T.sem.arrived, 16)
+    g.dma_start(T.y[:, :], T.land[:, :], accum_op=AluOpType.add).then_inc(T.sem.added, 16)
 
-    for k in range(NBLK):
-        g.wait_ge(T.sem["acc%d" % k], 16 * len(peers))
-    g.wait_ge(T.sem.sent, nsent)
+    g.wait_ge(T.sem.added, 16)
+    g.wait_ge(T.sem.sent, 16)

from concourse.mybir import AluOpType

SCRATCH = {
    "mine": ("sbuf", [128, 1024], "float32"),
    "land": ("sbuf", [128, 1024], "float32"),
}
SEMAPHORES = ["seed", "staged", "sent", "arrived", "added"]


def rank_program(g, core, T, topo):
    rank = T.rank_of(core)
    if rank is None:
        return
    pair = [grp for grp in T.tables["GROUPS"] if rank in grp][0]
    partner = T.cores[[r for r in pair if r != rank][0]]
    rid, pid, _se = topo.addr(partner)

    g.scalar.dma_start(T.y[:, :], T.x[:, :]).then_inc(T.sem.seed, 16)

    g.sync.dma_start(T.mine[:, :], T.x[:, :]).then_inc(T.sem.staged, 16)
    g.wait_ge(T.sem.staged, 16)
    g.remote_dma(T.land[:, :], T.mine[:, :], T.sem.arrived, T.sem.sent, pid, rid, topo.mask(core, partner))

    g.wait_ge(T.sem.seed, 16)
    g.wait_ge(T.sem.arrived, 16)
    g.dma_start(T.y[:, :], T.land[:, :], accum_op=AluOpType.add).then_inc(T.sem.added, 16)

    g.wait_ge(T.sem.added, 16)
    g.wait_ge(T.sem.sent, 16)
